import numpy as np
import ml_dtypes


def mxq(x, axis, fmt="e4m3"):
    dtype, down = {"e4m3": (ml_dtypes.float8_e4m3fn, 7), "e5m2": (ml_dtypes.float8_e5m2, 14)}[fmt]
    v = np.moveaxis(np.asarray(x, np.float32).astype(ml_dtypes.bfloat16).astype(np.float64), axis, -1)
    blocks = v.reshape(v.shape[:-1] + (-1, 32))
    amax = np.abs(blocks).max(-1, keepdims=True)
    byte = np.maximum(np.where(amax > 0, np.frexp(amax)[1] - 1 + 127, 0) - down, 1)
    scale = np.exp2(byte - 127.0)
    codes = (blocks / scale).astype(np.float32).astype(dtype).astype(np.float64)
    return np.moveaxis((codes * scale).reshape(v.shape), -1, axis)


WIDE = False


def mx_kscale(k):
    if not WIDE:
        return np.ones(k)
    levels = np.array([10, -10, 5, -5, 0])
    if k % 512:
        return np.exp2(np.random.permutation(np.resize(levels, k // 32))).repeat(32)
    a = np.empty((k // 512, 16))
    for p in range(k // 512):
        a[p, :8] = np.random.permutation(np.resize(levels, 8))
        for g in range(8):
            far = levels[np.abs(levels - a[p, g]) >= 10]
            a[p, g + 8] = far[np.random.randint(len(far))]
    return np.exp2(a.ravel()).repeat(32)


def f64(x):
    return np.asarray(x).astype(np.float64)


def striped(idx):
    return np.tile(idx.reshape(-1, 16).T, (8, 1)).astype(np.uint16)


def unstriped(offs):
    return offs[:16].T.reshape(-1).astype(np.int64)


E2M1 = np.array([0.0, 0.5, 1.0, 1.5, 2.0, 3.0, 4.0, 6.0, -0.0, -0.5, -1.0, -1.5, -2.0, -3.0, -4.0, -6.0])


def pack_weight(w, fmt):
    k, n = w.shape
    w = f64(np.asarray(w, np.float32).astype(ml_dtypes.bfloat16)).reshape(k // 32, 32, n)
    amax = np.abs(w).max(1)
    if fmt == "e4m3":
        byte = np.frexp(amax)[1] - 1 + 127 - 7
    else:
        mant, ex = np.frexp(amax / 6.0)
        byte = np.where(mant > 0.5, ex, ex - 1) + 127
    byte = np.clip(np.where(amax > 0, byte, 1), 1, 254)
    scaled = (w * np.exp2(127.0 - byte)[:, None, :]).reshape(k, n).astype(np.float32)
    by_word = np.ascontiguousarray(scaled.reshape(k // 512, 128, 4, n).transpose(0, 1, 3, 2))
    if fmt == "e4m3":
        words = by_word.astype(ml_dtypes.float8_e4m3fn).view(np.uint8)
    else:
        c = by_word.astype(ml_dtypes.float4_e2m1fn).view(np.uint8) & 0xF
        words = (c[..., 0::2] | (c[..., 1::2] << 4)).reshape(k // 512, 128, 2 * n)
    return np.ascontiguousarray(words), np.ascontiguousarray(byte.astype(np.uint8).reshape(k // 512, 16, n))


def unpack_weight(words, scales, fmt):
    g, _, n = scales.shape
    words = np.ascontiguousarray(words).reshape(g, 128, n, -1)
    if fmt == "e4m3":
        vals = words.view(ml_dtypes.float8_e4m3fn).astype(np.float64)
    else:
        nib = np.empty((g, 128, n, 4), np.uint8)
        nib[..., 0::2] = words & 0xF
        nib[..., 1::2] = words >> 4
        vals = E2M1[nib]
    vals = vals * np.repeat(np.exp2(scales.astype(np.float64) - 127.0), 8, axis=1)[..., None]
    return vals.transpose(0, 1, 3, 2).reshape(g * 512, n)


def relu2(v):
    return np.maximum(v, 0.0) ** 2


K, T, E, C, N = 1024, 1536, 8, 128, 512


def by_expert(wq, xq):
    return np.concatenate([wq[e].T @ xq[:, e * C:(e + 1) * C] for e in range(E)], axis=1)


def setup_inputs():
    n = np.random.standard_normal
    s = mx_kscale(K)[:, None]
    w = [pack_weight(m, "e2m1") for m in n((E, K, N)) / np.sqrt(K) / s[None]]
    return {
        "xT": (n((K, T)) * s).astype(np.float32),
        "w_words": np.stack([m[0] for m in w]),
        "w_scales": np.stack([m[1] for m in w]),
        "b": (0.3 * n((N, E))).astype(np.float32),
        "gate": np.tile(np.random.uniform(0.2, 1.0, E * C), (N, 1)).astype(np.float32),
        "offs": striped(np.random.permutation(T)[:E * C]),
        "dst": striped(np.random.permutation(T)[:E * C]),
    }


def reference(xT, w_words, w_scales, b, gate, offs, dst):
    idx = unstriped(offs)
    w = np.stack([unpack_weight(w_words[e], w_scales[e], "e2m1") for e in range(E)])
    xq = mxq(f64(xT)[:, idx], 0, "e4m3")
    y = by_expert(w, xq)
    y = relu2(y + np.repeat(f64(b), C, axis=1))
    out = np.zeros((N, T))
    out[:, unstriped(dst)] = f64(gate) * y
    return out

@@ -1,0 +1,160 @@
+from contextlib import ExitStack
+
+import concourse.mybir as mybir
+
+K, T, E, C, N = 1024, 1536, 8, 128, 512
+S = E * C
+P = 128
+PACK = 4
+PASSES = K // (P * PACK)
+N_TILES = N // P
+CHUNK = 512
+PAIR = 2 * C
+
+FLOPS = 2 * K * S * N
+BYTES = 4 * K * T + E * PASSES * (P * 2 * N + 16 * N) + 4 * N * E + 4 * S + 2 * 2 * P * (S // 16) + 4 * N * T
+
+F32 = mybir.dt.float32
+BF16 = mybir.dt.bfloat16
+I32 = mybir.dt.int32
+U32 = mybir.dt.uint32
+U16 = mybir.dt.uint16
+U8 = mybir.dt.uint8
+E4M3X4 = mybir.dt.float8_e4m3fn_x4
+E2M1X4 = mybir.dt.float4_e2m1fn_x4
+ACT = mybir.ActivationFunctionType
+MULT = mybir.AluOpType.mult
+
+SCALAR_COLS = {(1, 2): 176}
+
+
+def tile_moe_two_lin_relu2_kernel(tc, xT, w_words, w_scales, b, gate, offs, dst, out):
+    nc = tc.nc
+    with ExitStack() as ctx:
+        keep = ctx.enter_context(tc.tile_pool(name="keep", bufs=1))
+        raws = ctx.enter_context(tc.tile_pool(name="raws", bufs=6))
+        work = ctx.enter_context(tc.tile_pool(name="work", bufs=4))
+        psum = ctx.enter_context(tc.psum_pool(name="psum", bufs=8))
+
+        offs_sb = keep.tile([P, S // 16], U16, name="offs_sb")
+        dst_sb = keep.tile([P, S // 16], U16, name="dst_sb")
+        b_sb = keep.tile([P, N_TILES, E], F32, name="b_sb")
+        gate_sb = keep.tile([P, S], F32, name="gate_sb")
+        w_sb = [keep.tile([P, PASSES, 2 * N], U8, name=f"w_sb{e}", align_bytes=64) for e in range(E)]
+        ws_sb = keep.tile([P, E * PASSES, N], U8, name="ws_sb", align_bytes=64)
+        codes = [keep.tile([P, T], U32, name=f"codes{a}", align_bytes=64) for a in range(PASSES)]
+        bytes_ = [keep.tile([P, T], U8, name=f"scale_bytes{a}", align_bytes=64) for a in range(PASSES)]
+        outs = [keep.tile([P, T], F32, name=f"out_sb{t}") for t in range(N_TILES)]
+
+        nc.scalar.dma_start(out=b_sb[:], in_=b.rearrange("(t p) e -> p t e", p=P))
+
+        raw = {}
+        for a in range(PASSES):
+            rows = xT[a * 512 : (a + 1) * 512, :].rearrange("(p d) t -> p d t", d=PACK)
+            for c in range(T // CHUNK):
+                r = raws.tile([P, PACK, CHUNK], F32, name="raw")
+                nc.sync.dma_start(out=r[:], in_=rows[:, :, c * CHUNK : (c + 1) * CHUNK])
+                raw[a, c] = r
+                if (a, c) == (0, 1):
+                    nc.sync.dma_start(offs_sb[:], offs)
+                    nc.sync.dma_start(dst_sb[:], dst)
+
+        nc.gpsimd.memset(bytes_[0][:].bitcast(I32), 0)
+        nc.gpsimd.memset(bytes_[1][:].bitcast(I32), 0)
+        nc.vector.memset(ws_sb[:].rearrange("p g n -> p (g n)").bitcast(I32), 0)
+        for t in range(N_TILES):
+            (nc.vector if t < 2 else nc.gpsimd).memset(outs[t][:], 0.0)
+
+        def load_w(e):
+            nc.sync.dma_start(out=w_sb[e][:].bitcast(I32), in_=w_words[e].rearrange("a p c -> p a c").bitcast(I32))
+
+        def load_ws(e0, e1):
+            for q in range(4):
+                nc.sync.dma_start(
+                    out=ws_sb[32 * q : 32 * q + 4, 2 * e0 : 2 * e1, :].bitcast(I32),
+                    in_=w_scales[e0:e1, :, 4 * q : 4 * q + 4, :].rearrange("e a r n -> r (e a) n").bitcast(I32),
+                )
+
+        load_w(0)
+        load_ws(0, 2)
+        load_w(1)
+        nc.sync.dma_start(gate_sb[:], gate[0:P, :])
+        load_w(2)
+        load_ws(2, 8)
+        for e in range(3, E):
+            load_w(e)
+
+        def prepare(a, c):
+            split = SCALAR_COLS.get((a, c), 384)
+            g = work.tile([P, CHUNK, PACK], BF16, name="grouped", align_bytes=64)
+            src = raw[a, c][:].rearrange("p d t -> p t d")
+            nc.scalar.copy(g[:, 0:split, :], src[:, 0:split, :])
+            nc.vector.tensor_copy(g[:, split:CHUNK, :], src[:, split:CHUNK, :])
+            cols = slice(c * CHUNK, (c + 1) * CHUNK)
+            nc.vector.quantize_mx(
+                out=codes[a][:, cols].bitcast(E4M3X4),
+                scales=bytes_[a][:, cols],
+                in_=g[:].rearrange("p t d -> p (t d)"),
+            )
+
+        for c in range(3):
+            prepare(0, c)
+        gw0 = keep.tile([P, S], U32, name="gw0", align_bytes=64)
+        gs0 = keep.tile([P, S], U8, name="gs0", align_bytes=64)
+        prepare(1, 0)
+        nc.vector.tensor_copy(gw0[:], codes[0][:].indirect(offs_sb[:]))
+        prepare(1, 1)
+        nc.vector.tensor_copy(gs0[:], bytes_[0][:].indirect(offs_sb[:]))
+        prepare(1, 2)
+
+        gw1 = []
+        gs1 = []
+
+        def gather1(pr):
+            cols = offs_sb[:, pr * (PAIR // 16) : (pr + 1) * (PAIR // 16)]
+            w = keep.tile([P, PAIR], U32, name=f"gw1_{pr}", align_bytes=64)
+            s = keep.tile([P, PAIR], U8, name=f"gs1_{pr}", align_bytes=64)
+            nc.vector.tensor_copy(w[:], codes[1][:].indirect(cols))
+            nc.vector.tensor_copy(s[:], bytes_[1][:].indirect(cols))
+            gw1.append(w)
+            gs1.append(s)
+
+        def produce(t, pr):
+            acc = psum.tile([P, PAIR], F32, name="acc")
+            u = work.tile([P, PAIR], F32, name="u")
+            n_cols = slice(t * P, (t + 1) * P)
+            for i in range(2):
+                e = 2 * pr + i
+                sl = slice(i * C, (i + 1) * C)
+                for a in range(PASSES):
+                    rhs = gw0[:, e * C : (e + 1) * C] if a == 0 else gw1[pr][:, sl]
+                    rhs_scale = gs0[:, e * C : (e + 1) * C] if a == 0 else gs1[pr][:, sl]
+                    nc.tensor.matmul_mx(
+                        out=acc[:, sl],
+                        lhsT=w_sb[e][:, a, t * 2 * P : (t + 1) * 2 * P].bitcast(E2M1X4),
+                        lhsT_scale=ws_sb[:, 2 * e + a, n_cols],
+                        rhs=rhs.bitcast(E4M3X4),
+                        rhs_scale=rhs_scale,
+                        start=(a == 0),
+                        stop=(a == PASSES - 1),
+                    )
+                nc.scalar.activation(u[:, sl], acc[:, sl], ACT.Relu, bias=b_sb[:, t, e : e + 1])
+            sq = work.tile([P, PAIR], F32, name="sq")
+            nc.scalar.activation(sq[:], u[:], ACT.Square)
+            m = work.tile([P, PAIR], F32, name="m")
+            nc.gpsimd.tensor_tensor(m[:], sq[:], gate_sb[:, pr * PAIR : (pr + 1) * PAIR], MULT)
+            return m
+
+        def scatter(t, pr, m):
+            nc.vector.tensor_copy(outs[t][:].indirect(dst_sb[:, pr * (PAIR // 16) : (pr + 1) * (PAIR // 16)]), m[:])
+
+        gather1(0)
+        gather1(1)
+        gather1(2)
+        for t in range(N_TILES):
+            for pr in range(4):
+                m = produce(t, pr)
+                scatter(t, pr, m)
+                if (t, pr) == (0, 0):
+                    gather1(3)
+            nc.sync.dma_start(out=out[t * P : (t + 1) * P, :], in_=outs[t][:])

@@ -8,8 +8,7 @@ P = 128
 PACK = 4
 PASSES = K // (P * PACK)
 N_TILES = N // P
-CHUNK = 512
-PAIR = 2 * C
+CHUNKS = (((0, 512), (512, 1024), (1024, 1536)), ((0, 512), (512, 1024), (1024, 1280), (1280, 1536)))
 
 FLOPS = 2 * K * S * N
 BYTES = 4 * K * T + E * PASSES * (P * 2 * N + 16 * N) + 4 * N * E + 4 * S + 2 * 2 * P * (S // 16) + 4 * N * T
@@ -25,14 +24,14 @@ E2M1X4 = mybir.dt.float4_e2m1fn_x4
 ACT = mybir.ActivationFunctionType
 MULT = mybir.AluOpType.mult
 
-SCALAR_COLS = {(1, 2): 176}
+SCALAR_COLS = ((192, 192, 192), (512, 384, 256, 96))
+HALF = 4 * C
 
 
 def tile_moe_two_lin_relu2_kernel(tc, xT, w_words, w_scales, b, gate, offs, dst, out):
     nc = tc.nc
     with ExitStack() as ctx:
         keep = ctx.enter_context(tc.tile_pool(name="keep", bufs=1))
-        raws = ctx.enter_context(tc.tile_pool(name="raws", bufs=6))
         work = ctx.enter_context(tc.tile_pool(name="work", bufs=4))
         psum = ctx.enter_context(tc.psum_pool(name="psum", bufs=8))
 
@@ -40,7 +39,7 @@ def tile_moe_two_lin_relu2_kernel(tc, xT, w_words, w_scales, b, gate, offs, dst,
         dst_sb = keep.tile([P, S // 16], U16, name="dst_sb")
         b_sb = keep.tile([P, N_TILES, E], F32, name="b_sb")
         gate_sb = keep.tile([P, S], F32, name="gate_sb")
-        w_sb = [keep.tile([P, PASSES, 2 * N], U8, name=f"w_sb{e}", align_bytes=64) for e in range(E)]
+        w_sb = [keep.tile([P, 2 * PASSES, 2 * N], U8, name=f"w_sb{g}", align_bytes=64) for g in range(E // 2)]
         ws_sb = keep.tile([P, E * PASSES, N], U8, name="ws_sb", align_bytes=64)
         codes = [keep.tile([P, T], U32, name=f"codes{a}", align_bytes=64) for a in range(PASSES)]
         bytes_ = [keep.tile([P, T], U8, name=f"scale_bytes{a}", align_bytes=64) for a in range(PASSES)]
@@ -51,22 +50,26 @@ def tile_moe_two_lin_relu2_kernel(tc, xT, w_words, w_scales, b, gate, offs, dst,
         raw = {}
         for a in range(PASSES):
             rows = xT[a * 512 : (a + 1) * 512, :].rearrange("(p d) t -> p d t", d=PACK)
-            for c in range(T // CHUNK):
-                r = raws.tile([P, PACK, CHUNK], F32, name="raw")
-                nc.sync.dma_start(out=r[:], in_=rows[:, :, c * CHUNK : (c + 1) * CHUNK])
+            for c, (t0, t1) in enumerate(CHUNKS[a]):
+                r = keep.tile([P, PACK, t1 - t0], F32, name=f"raw{a}_{c}")
+                nc.sync.dma_start(out=r[:], in_=rows[:, :, t0:t1])
                 raw[a, c] = r
                 if (a, c) == (0, 1):
                     nc.sync.dma_start(offs_sb[:], offs)
                     nc.sync.dma_start(dst_sb[:], dst)
 
         nc.gpsimd.memset(bytes_[0][:].bitcast(I32), 0)
+        nc.vector.memset(outs[0][:], 0.0)
+        nc.vector.memset(outs[1][:], 0.0)
+        nc.gpsimd.memset(outs[2][:], 0.0)
         nc.gpsimd.memset(bytes_[1][:].bitcast(I32), 0)
-        nc.vector.memset(ws_sb[:].rearrange("p g n -> p (g n)").bitcast(I32), 0)
-        for t in range(N_TILES):
-            (nc.vector if t < 2 else nc.gpsimd).memset(outs[t][:], 0.0)
+        nc.gpsimd.memset(ws_sb[:].rearrange("p g n -> p (g n)").bitcast(I32), 0)
+        nc.gpsimd.memset(outs[3][:], 0.0)
 
-        def load_w(e):
-            nc.sync.dma_start(out=w_sb[e][:].bitcast(I32), in_=w_words[e].rearrange("a p c -> p a c").bitcast(I32))
+        def load_w(g):
+            nc.sync.dma_start(
+                out=w_sb[g][:].bitcast(I32), in_=w_words[2 * g : 2 * g + 2].rearrange("e a p c -> p (e a) c").bitcast(I32)
+            )
 
         def load_ws(e0, e1):
             for q in range(4):
@@ -76,21 +79,24 @@ def tile_moe_two_lin_relu2_kernel(tc, xT, w_words, w_scales, b, gate, offs, dst,
                 )
 
         load_w(0)
-        load_ws(0, 2)
+        load_ws(0, 4)
         load_w(1)
         nc.sync.dma_start(gate_sb[:], gate[0:P, :])
         load_w(2)
-        load_ws(2, 8)
-        for e in range(3, E):
-            load_w(e)
+        load_ws(4, 8)
+        load_w(3)
 
         def prepare(a, c):
-            split = SCALAR_COLS.get((a, c), 384)
-            g = work.tile([P, CHUNK, PACK], BF16, name="grouped", align_bytes=64)
+            t0, t1 = CHUNKS[a][c]
+            width = t1 - t0
+            split = SCALAR_COLS[a][c]
+            g = work.tile([P, width, PACK], BF16, name="grouped", align_bytes=64)
             src = raw[a, c][:].rearrange("p d t -> p t d")
-            nc.scalar.copy(g[:, 0:split, :], src[:, 0:split, :])
-            nc.vector.tensor_copy(g[:, split:CHUNK, :], src[:, split:CHUNK, :])
-            cols = slice(c * CHUNK, (c + 1) * CHUNK)
+            if split:
+                nc.scalar.copy(g[:, 0:split, :], src[:, 0:split, :])
+            if split < width:
+                nc.vector.tensor_copy(g[:, split:width, :], src[:, split:width, :])
+            cols = slice(t0, t1)
             nc.vector.quantize_mx(
                 out=codes[a][:, cols].bitcast(E4M3X4),
                 scales=bytes_[a][:, cols],
@@ -106,55 +112,55 @@ def tile_moe_two_lin_relu2_kernel(tc, xT, w_words, w_scales, b, gate, offs, dst,
         prepare(1, 1)
         nc.vector.tensor_copy(gs0[:], bytes_[0][:].indirect(offs_sb[:]))
         prepare(1, 2)
+        prepare(1, 3)
 
-        gw1 = []
-        gs1 = []
+        gw1 = keep.tile([P, S], U32, name="gw1", align_bytes=64)
+        gs1 = keep.tile([P, S], U8, name="gs1", align_bytes=64)
+        for s0, s1 in ((0, 256), (256, 512), (512, 1024)):
+            cols = offs_sb[:, s0 // 16 : s1 // 16]
+            nc.vector.tensor_copy(gw1[:, s0:s1], codes[1][:].indirect(cols))
+            nc.vector.tensor_copy(gs1[:, s0:s1], bytes_[1][:].indirect(cols))
 
-        def gather1(pr):
-            cols = offs_sb[:, pr * (PAIR // 16) : (pr + 1) * (PAIR // 16)]
-            w = keep.tile([P, PAIR], U32, name=f"gw1_{pr}", align_bytes=64)
-            s = keep.tile([P, PAIR], U8, name=f"gs1_{pr}", align_bytes=64)
-            nc.vector.tensor_copy(w[:], codes[1][:].indirect(cols))
-            nc.vector.tensor_copy(s[:], bytes_[1][:].indirect(cols))
-            gw1.append(w)
-            gs1.append(s)
+        squares = [keep.tile([P, S], F32, name=f"squares{t}") for t in range(N_TILES)]
+        words = (gw0, gw1)
+        scales = (gs0, gs1)
 
-        def produce(t, pr):
-            acc = psum.tile([P, PAIR], F32, name="acc")
-            u = work.tile([P, PAIR], F32, name="u")
+        def produce(t, s0, s1):
+            acc = psum.tile([P, s1 - s0], F32, name="acc")
+            u = work.tile([P, s1 - s0], F32, name="u")
             n_cols = slice(t * P, (t + 1) * P)
-            for i in range(2):
-                e = 2 * pr + i
-                sl = slice(i * C, (i + 1) * C)
+            for e in range(s0 // C, s1 // C):
+                slots = slice(e * C, (e + 1) * C)
+                local = slice(e * C - s0, (e + 1) * C - s0)
                 for a in range(PASSES):
-                    rhs = gw0[:, e * C : (e + 1) * C] if a == 0 else gw1[pr][:, sl]
-                    rhs_scale = gs0[:, e * C : (e + 1) * C] if a == 0 else gs1[pr][:, sl]
                     nc.tensor.matmul_mx(
-                        out=acc[:, sl],
-                        lhsT=w_sb[e][:, a, t * 2 * P : (t + 1) * 2 * P].bitcast(E2M1X4),
-                        lhsT_scale=ws_sb[:, 2 * e + a, n_cols],
-                        rhs=rhs.bitcast(E4M3X4),
-                        rhs_scale=rhs_scale,
+                        out=acc[:, local],
+                        lhsT=w_sb[e // 2][:, PASSES * (e % 2) + a, t * 2 * P : (t + 1) * 2 * P].bitcast(E2M1X4),
+                        lhsT_scale=ws_sb[:, PASSES * e + a, n_cols],
+                        rhs=words[a][:, slots].bitcast(E4M3X4),
+                        rhs_scale=scales[a][:, slots],
                         start=(a == 0),
                         stop=(a == PASSES - 1),
                     )
-                nc.scalar.activation(u[:, sl], acc[:, sl], ACT.Relu, bias=b_sb[:, t, e : e + 1])
-            sq = work.tile([P, PAIR], F32, name="sq")
-            nc.scalar.activation(sq[:], u[:], ACT.Square)
-            m = work.tile([P, PAIR], F32, name="m")
-            nc.gpsimd.tensor_tensor(m[:], sq[:], gate_sb[:, pr * PAIR : (pr + 1) * PAIR], MULT)
-            return m
+                nc.scalar.activation(u[:, local], acc[:, local], ACT.Relu, bias=b_sb[:, t, e : e + 1])
+            nc.scalar.activation(squares[t][:, s0:s1], u[:], ACT.Square)
 
-        def scatter(t, pr, m):
-            nc.vector.tensor_copy(outs[t][:].indirect(dst_sb[:, pr * (PAIR // 16) : (pr + 1) * (PAIR // 16)]), m[:])
+        def scatter(t, s0, s1):
+            nc.vector.tensor_tensor(
+                outs[t][:].indirect(dst_sb[:, s0 // 16 : s1 // 16]), squares[t][:, s0:s1], gate_sb[:, s0:s1], MULT
+            )
 
-        gather1(0)
-        gather1(1)
-        gather1(2)
-        for t in range(N_TILES):
-            for pr in range(4):
-                m = produce(t, pr)
-                scatter(t, pr, m)
-                if (t, pr) == (0, 0):
-                    gather1(3)
+        def store(t):
             nc.sync.dma_start(out=out[t * P : (t + 1) * P, :], in_=outs[t][:])
+
+        for s0, s1 in ((0, 256), (256, 512), (512, 1024)):
+            for t in (0, 1):
+                produce(t, s0, s1)
+                scatter(t, s0, s1)
+                if s1 == S:
+                    store(t)
+        for t in (2, 3):
+            produce(t, 0, 512)
+            produce(t, 512, 1024)
+            scatter(t, 0, S)
+            store(t)

@@ -41,11 +41,9 @@ def tile_moe_two_lin_relu2_kernel(tc, xT, w_words, w_scales, b, gate, offs, dst,
         gate_sb = keep.tile([P, S], F32, name="gate_sb")
         w_sb = [keep.tile([P, 2 * PASSES, 2 * N], U8, name=f"w_sb{g}", align_bytes=64) for g in range(E // 2)]
         ws_sb = keep.tile([P, E * PASSES, N], U8, name="ws_sb", align_bytes=64)
-        codes = [keep.tile([P, T], U32, name=f"codes{a}", align_bytes=64) for a in range(PASSES)]
-        bytes_ = [keep.tile([P, T], U8, name=f"scale_bytes{a}", align_bytes=64) for a in range(PASSES)]
-        outs = [keep.tile([P, T], F32, name=f"out_sb{t}") for t in range(N_TILES)]
-
-        nc.scalar.dma_start(out=b_sb[:], in_=b.rearrange("(t p) e -> p t e", p=P))
+        codes = [keep.tile([P, T], U32, name=f"codes{a}", tag=f"codes{a}", align_bytes=64) for a in range(PASSES)]
+        bytes_ = [keep.tile([P, T], U8, name=f"scale_bytes{a}", tag=f"scale_bytes{a}", align_bytes=64) for a in range(PASSES)]
+        outs = [keep.tile([P, T], F32, name=f"out_sb{t}") for t in range(2)]
 
         raw = {}
         for a in range(PASSES):
@@ -56,15 +54,15 @@ def tile_moe_two_lin_relu2_kernel(tc, xT, w_words, w_scales, b, gate, offs, dst,
                 raw[a, c] = r
                 if (a, c) == (0, 1):
                     nc.sync.dma_start(offs_sb[:], offs)
-                    nc.sync.dma_start(dst_sb[:], dst)
 
         nc.gpsimd.memset(bytes_[0][:].bitcast(I32), 0)
         nc.vector.memset(outs[0][:], 0.0)
         nc.vector.memset(outs[1][:], 0.0)
-        nc.gpsimd.memset(outs[2][:], 0.0)
         nc.gpsimd.memset(bytes_[1][:].bitcast(I32), 0)
         nc.gpsimd.memset(ws_sb[:].rearrange("p g n -> p (g n)").bitcast(I32), 0)
-        nc.gpsimd.memset(outs[3][:], 0.0)
+        warm = keep.tile([P, 1], F32, name="warm")
+        nc.gpsimd.memset(warm[:], 0.0)
+        nc.scalar.activation(warm[:], warm[:], ACT.Square)
 
         def load_w(g):
             nc.sync.dma_start(
@@ -80,7 +78,9 @@ def tile_moe_two_lin_relu2_kernel(tc, xT, w_words, w_scales, b, gate, offs, dst,
 
         load_w(0)
         load_ws(0, 4)
+        nc.sync.dma_start(out=b_sb[:], in_=b.rearrange("(t p) e -> p t e", p=P))
         load_w(1)
+        nc.sync.dma_start(dst_sb[:], dst)
         nc.sync.dma_start(gate_sb[:], gate[0:P, :])
         load_w(2)
         load_ws(4, 8)
@@ -120,6 +120,11 @@ def tile_moe_two_lin_relu2_kernel(tc, xT, w_words, w_scales, b, gate, offs, dst,
             cols = offs_sb[:, s0 // 16 : s1 // 16]
             nc.vector.tensor_copy(gw1[:, s0:s1], codes[1][:].indirect(cols))
             nc.vector.tensor_copy(gs1[:, s0:s1], bytes_[1][:].indirect(cols))
+
+        for t, tag in ((2, "codes1"), (3, "scale_bytes1")):
+            o = keep.tile([P, T], F32, name=f"out_sb{t}", tag=tag, align_bytes=64)
+            nc.gpsimd.memset(o[:], 0.0)
+            outs.append(o)
 
         squares = [keep.tile([P, S], F32, name=f"squares{t}") for t in range(N_TILES)]
         words = (gw0, gw1)

@@ -8,7 +8,7 @@ P = 128
 PACK = 4
 PASSES = K // (P * PACK)
 N_TILES = N // P
-CHUNKS = (((0, 512), (512, 1024), (1024, 1536)), ((0, 512), (512, 1024), (1024, 1280), (1280, 1536)))
+CHUNKS = (((0, 768), (768, 1280), (1280, 1536)), ((0, 512), (512, 1024), (1024, 1280), (1280, 1536)))
 
 FLOPS = 2 * K * S * N
 BYTES = 4 * K * T + E * PASSES * (P * 2 * N + 16 * N) + 4 * N * E + 4 * S + 2 * 2 * P * (S // 16) + 4 * N * T
@@ -24,7 +24,7 @@ E2M1X4 = mybir.dt.float4_e2m1fn_x4
 ACT = mybir.ActivationFunctionType
 MULT = mybir.AluOpType.mult
 
-SCALAR_COLS = ((192, 192, 192), (512, 384, 256, 96))
+SCALAR_COLS = ((352, 256, 96), (512, 416, 192, 96))
 HALF = 4 * C
 
 
@@ -70,38 +70,48 @@ def tile_moe_two_lin_relu2_kernel(tc, xT, w_words, w_scales, b, gate, offs, dst,
             )
 
         def load_ws(e0, e1):
-            for q in range(4):
+            for r in range(4):
                 nc.sync.dma_start(
-                    out=ws_sb[32 * q : 32 * q + 4, 2 * e0 : 2 * e1, :].bitcast(I32),
-                    in_=w_scales[e0:e1, :, 4 * q : 4 * q + 4, :].rearrange("e a r n -> r (e a) n").bitcast(I32),
+                    out=ws_sb[r : P : 32, 2 * e0 : 2 * e1, :].bitcast(I32),
+                    in_=w_scales[e0:e1, :, r : 16 : 4, :].rearrange("e a q n -> q (e a) n").bitcast(I32),
                 )
 
-        load_w(0)
         load_ws(0, 4)
+        load_w(0)
         nc.sync.dma_start(out=b_sb[:], in_=b.rearrange("(t p) e -> p t e", p=P))
         load_w(1)
         nc.sync.dma_start(dst_sb[:], dst)
-        nc.sync.dma_start(gate_sb[:], gate[0:P, :])
-        load_w(2)
+        nc.sync.dma_start(gate_sb[:, 0:HALF], gate[0:P, 0:HALF])
         load_ws(4, 8)
+        load_w(2)
         load_w(3)
+        nc.sync.dma_start(gate_sb[:, HALF:S], gate[0:P, HALF:S])
 
         def prepare(a, c):
             t0, t1 = CHUNKS[a][c]
             width = t1 - t0
             split = SCALAR_COLS[a][c]
             g = work.tile([P, width, PACK], BF16, name="grouped", align_bytes=64)
-            src = raw[a, c][:].rearrange("p d t -> p t d")
+            src = raw[a, c]
+
+            def four(lo, hi):
+                return (
+                    g[:, lo:hi, :].rearrange("p (c i) d -> p c d i", i=4),
+                    src[:, :, lo:hi].rearrange("p d (c i) -> p c d i", i=4),
+                )
+
             if split:
-                nc.scalar.copy(g[:, 0:split, :], src[:, 0:split, :])
+                nc.scalar.copy(*four(0, split))
             if split < width:
-                nc.vector.tensor_copy(g[:, split:width, :], src[:, split:width, :])
-            cols = slice(t0, t1)
-            nc.vector.quantize_mx(
-                out=codes[a][:, cols].bitcast(E4M3X4),
-                scales=bytes_[a][:, cols],
-                in_=g[:].rearrange("p t d -> p (t d)"),
-            )
+                nc.vector.tensor_copy(*four(split, width))
+            for lo in range(0, width, 512):
+                hi = min(lo + 512, width)
+                cols = slice(t0 + lo, t0 + hi)
+                nc.vector.quantize_mx(
+                    out=codes[a][:, cols].bitcast(E4M3X4),
+                    scales=bytes_[a][:, cols],
+                    in_=g[:, lo:hi, :].rearrange("p t d -> p (t d)"),
+                )
 
         for c in range(3):
             prepare(0, c)
@@ -116,7 +126,7 @@ def tile_moe_two_lin_relu2_kernel(tc, xT, w_words, w_scales, b, gate, offs, dst,
 
         gw1 = keep.tile([P, S], U32, name="gw1", align_bytes=64)
         gs1 = keep.tile([P, S], U8, name="gs1", align_bytes=64)
-        for s0, s1 in ((0, 256), (256, 512), (512, 1024)):
+        for s0, s1 in ((0, 512), (512, 1024)):
             cols = offs_sb[:, s0 // 16 : s1 // 16]
             nc.vector.tensor_copy(gw1[:, s0:s1], codes[1][:].indirect(cols))
             nc.vector.tensor_copy(gs1[:, s0:s1], bytes_[1][:].indirect(cols))

@@ -24,7 +24,7 @@ E2M1X4 = mybir.dt.float4_e2m1fn_x4
 ACT = mybir.ActivationFunctionType
 MULT = mybir.AluOpType.mult
 
-SCALAR_COLS = ((352, 256, 96), (512, 416, 192, 96))
+SCALAR_COLS = ((352, 256, 96), (512, 512, 256, 96))
 HALF = 4 * C
 
 
@@ -79,9 +79,9 @@ def tile_moe_two_lin_relu2_kernel(tc, xT, w_words, w_scales, b, gate, offs, dst,
         load_ws(0, 4)
         load_w(0)
         nc.sync.dma_start(out=b_sb[:], in_=b.rearrange("(t p) e -> p t e", p=P))
-        load_w(1)
         nc.sync.dma_start(dst_sb[:], dst)
         nc.sync.dma_start(gate_sb[:, 0:HALF], gate[0:P, 0:HALF])
+        load_w(1)
         load_ws(4, 8)
         load_w(2)
         load_w(3)
@@ -117,12 +117,10 @@ def tile_moe_two_lin_relu2_kernel(tc, xT, w_words, w_scales, b, gate, offs, dst,
             prepare(0, c)
         gw0 = keep.tile([P, S], U32, name="gw0", align_bytes=64)
         gs0 = keep.tile([P, S], U8, name="gs0", align_bytes=64)
-        prepare(1, 0)
         nc.vector.tensor_copy(gw0[:], codes[0][:].indirect(offs_sb[:]))
-        prepare(1, 1)
         nc.vector.tensor_copy(gs0[:], bytes_[0][:].indirect(offs_sb[:]))
-        prepare(1, 2)
-        prepare(1, 3)
+        for c in range(4):
+            prepare(1, c)
 
         gw1 = keep.tile([P, S], U32, name="gw1", align_bytes=64)
         gs1 = keep.tile([P, S], U8, name="gs1", align_bytes=64)

from contextlib import ExitStack

import concourse.mybir as mybir

K, T, E, C, N = 1024, 1536, 8, 128, 512
S = E * C
P = 128
PACK = 4
PASSES = K // (P * PACK)
N_TILES = N // P
CHUNKS = (((0, 768), (768, 1280), (1280, 1536)), ((0, 512), (512, 1024), (1024, 1280), (1280, 1536)))

FLOPS = 2 * K * S * N
BYTES = 4 * K * T + E * PASSES * (P * 2 * N + 16 * N) + 4 * N * E + 4 * S + 2 * 2 * P * (S // 16) + 4 * N * T

F32 = mybir.dt.float32
BF16 = mybir.dt.bfloat16
I32 = mybir.dt.int32
U32 = mybir.dt.uint32
U16 = mybir.dt.uint16
U8 = mybir.dt.uint8
E4M3X4 = mybir.dt.float8_e4m3fn_x4
E2M1X4 = mybir.dt.float4_e2m1fn_x4
ACT = mybir.ActivationFunctionType
MULT = mybir.AluOpType.mult

SCALAR_COLS = ((352, 256, 96), (512, 512, 256, 96))
HALF = 4 * C


def tile_moe_two_lin_relu2_kernel(tc, xT, w_words, w_scales, b, gate, offs, dst, out):
    nc = tc.nc
    with ExitStack() as ctx:
        keep = ctx.enter_context(tc.tile_pool(name="keep", bufs=1))
        work = ctx.enter_context(tc.tile_pool(name="work", bufs=4))
        psum = ctx.enter_context(tc.psum_pool(name="psum", bufs=8))

        offs_sb = keep.tile([P, S // 16], U16, name="offs_sb")
        dst_sb = keep.tile([P, S // 16], U16, name="dst_sb")
        b_sb = keep.tile([P, N_TILES, E], F32, name="b_sb")
        gate_sb = keep.tile([P, S], F32, name="gate_sb")
        w_sb = [keep.tile([P, 2 * PASSES, 2 * N], U8, name=f"w_sb{g}", align_bytes=64) for g in range(E // 2)]
        ws_sb = keep.tile([P, E * PASSES, N], U8, name="ws_sb", align_bytes=64)
        codes = [keep.tile([P, T], U32, name=f"codes{a}", tag=f"codes{a}", align_bytes=64) for a in range(PASSES)]
        bytes_ = [keep.tile([P, T], U8, name=f"scale_bytes{a}", tag=f"scale_bytes{a}", align_bytes=64) for a in range(PASSES)]
        outs = [keep.tile([P, T], F32, name=f"out_sb{t}") for t in range(2)]

        raw = {}
        for a in range(PASSES):
            rows = xT[a * 512 : (a + 1) * 512, :].rearrange("(p d) t -> p d t", d=PACK)
            for c, (t0, t1) in enumerate(CHUNKS[a]):
                r = keep.tile([P, PACK, t1 - t0], F32, name=f"raw{a}_{c}")
                nc.sync.dma_start(out=r[:], in_=rows[:, :, t0:t1])
                raw[a, c] = r
                if (a, c) == (0, 1):
                    nc.sync.dma_start(offs_sb[:], offs)

        nc.gpsimd.memset(bytes_[0][:].bitcast(I32), 0)
        nc.vector.memset(outs[0][:], 0.0)
        nc.vector.memset(outs[1][:], 0.0)
        nc.gpsimd.memset(bytes_[1][:].bitcast(I32), 0)
        nc.gpsimd.memset(ws_sb[:].rearrange("p g n -> p (g n)").bitcast(I32), 0)
        warm = keep.tile([P, 1], F32, name="warm")
        nc.gpsimd.memset(warm[:], 0.0)
        nc.scalar.activation(warm[:], warm[:], ACT.Square)

        def load_w(g):
            nc.sync.dma_start(
                out=w_sb[g][:].bitcast(I32), in_=w_words[2 * g : 2 * g + 2].rearrange("e a p c -> p (e a) c").bitcast(I32)
            )

        def load_ws(e0, e1):
            for r in range(4):
                nc.sync.dma_start(
                    out=ws_sb[r : P : 32, 2 * e0 : 2 * e1, :].bitcast(I32),
                    in_=w_scales[e0:e1, :, r : 16 : 4, :].rearrange("e a q n -> q (e a) n").bitcast(I32),
                )

        load_ws(0, 4)
        load_w(0)
        nc.sync.dma_start(out=b_sb[:], in_=b.rearrange("(t p) e -> p t e", p=P))
        nc.sync.dma_start(dst_sb[:], dst)
        nc.sync.dma_start(gate_sb[:, 0:HALF], gate[0:P, 0:HALF])
        load_w(1)
        load_ws(4, 8)
        load_w(2)
        load_w(3)
        nc.sync.dma_start(gate_sb[:, HALF:S], gate[0:P, HALF:S])

        def prepare(a, c):
            t0, t1 = CHUNKS[a][c]
            width = t1 - t0
            split = SCALAR_COLS[a][c]
            g = work.tile([P, width, PACK], BF16, name="grouped", align_bytes=64)
            src = raw[a, c]

            def four(lo, hi):
                return (
                    g[:, lo:hi, :].rearrange("p (c i) d -> p c d i", i=4),
                    src[:, :, lo:hi].rearrange("p d (c i) -> p c d i", i=4),
                )

            if split:
                nc.scalar.copy(*four(0, split))
            if split < width:
                nc.vector.tensor_copy(*four(split, width))
            for lo in range(0, width, 512):
                hi = min(lo + 512, width)
                cols = slice(t0 + lo, t0 + hi)
                nc.vector.quantize_mx(
                    out=codes[a][:, cols].bitcast(E4M3X4),
                    scales=bytes_[a][:, cols],
                    in_=g[:, lo:hi, :].rearrange("p t d -> p (t d)"),
                )

        for c in range(3):
            prepare(0, c)
        gw0 = keep.tile([P, S], U32, name="gw0", align_bytes=64)
        gs0 = keep.tile([P, S], U8, name="gs0", align_bytes=64)
        nc.vector.tensor_copy(gw0[:], codes[0][:].indirect(offs_sb[:]))
        nc.vector.tensor_copy(gs0[:], bytes_[0][:].indirect(offs_sb[:]))
        for c in range(4):
            prepare(1, c)

        gw1 = keep.tile([P, S], U32, name="gw1", align_bytes=64)
        gs1 = keep.tile([P, S], U8, name="gs1", align_bytes=64)
        for s0, s1 in ((0, 512), (512, 1024)):
            cols = offs_sb[:, s0 // 16 : s1 // 16]
            nc.vector.tensor_copy(gw1[:, s0:s1], codes[1][:].indirect(cols))
            nc.vector.tensor_copy(gs1[:, s0:s1], bytes_[1][:].indirect(cols))

        for t, tag in ((2, "codes1"), (3, "scale_bytes1")):
            o = keep.tile([P, T], F32, name=f"out_sb{t}", tag=tag, align_bytes=64)
            nc.gpsimd.memset(o[:], 0.0)
            outs.append(o)

        squares = [keep.tile([P, S], F32, name=f"squares{t}") for t in range(N_TILES)]
        words = (gw0, gw1)
        scales = (gs0, gs1)

        def produce(t, s0, s1):
            acc = psum.tile([P, s1 - s0], F32, name="acc")
            u = work.tile([P, s1 - s0], F32, name="u")
            n_cols = slice(t * P, (t + 1) * P)
            for e in range(s0 // C, s1 // C):
                slots = slice(e * C, (e + 1) * C)
                local = slice(e * C - s0, (e + 1) * C - s0)
                for a in range(PASSES):
                    nc.tensor.matmul_mx(
                        out=acc[:, local],
                        lhsT=w_sb[e // 2][:, PASSES * (e % 2) + a, t * 2 * P : (t + 1) * 2 * P].bitcast(E2M1X4),
                        lhsT_scale=ws_sb[:, PASSES * e + a, n_cols],
                        rhs=words[a][:, slots].bitcast(E4M3X4),
                        rhs_scale=scales[a][:, slots],
                        start=(a == 0),
                        stop=(a == PASSES - 1),
                    )
                nc.scalar.activation(u[:, local], acc[:, local], ACT.Relu, bias=b_sb[:, t, e : e + 1])
            nc.scalar.activation(squares[t][:, s0:s1], u[:], ACT.Square)

        def scatter(t, s0, s1):
            nc.vector.tensor_tensor(
                outs[t][:].indirect(dst_sb[:, s0 // 16 : s1 // 16]), squares[t][:, s0:s1], gate_sb[:, s0:s1], MULT
            )

        def store(t):
            nc.sync.dma_start(out=out[t * P : (t + 1) * P, :], in_=outs[t][:])

        for s0, s1 in ((0, 256), (256, 512), (512, 1024)):
            for t in (0, 1):
                produce(t, s0, s1)
                scatter(t, s0, s1)
                if s1 == S:
                    store(t)
        for t in (2, 3):
            produce(t, 0, 512)
            produce(t, 512, 1024)
            scatter(t, 0, S)
            store(t)
